import numpy as np
import ml_dtypes


def mxq(x, axis, fmt="e4m3"):
    dtype, down = {"e4m3": (ml_dtypes.float8_e4m3fn, 7), "e5m2": (ml_dtypes.float8_e5m2, 14)}[fmt]
    v = np.moveaxis(np.asarray(x, np.float32).astype(ml_dtypes.bfloat16).astype(np.float64), axis, -1)
    blocks = v.reshape(v.shape[:-1] + (-1, 32))
    amax = np.abs(blocks).max(-1, keepdims=True)
    byte = np.maximum(np.where(amax > 0, np.frexp(amax)[1] - 1 + 127, 0) - down, 1)
    scale = np.exp2(byte - 127.0)
    codes = (blocks / scale).astype(np.float32).astype(dtype).astype(np.float64)
    return np.moveaxis((codes * scale).reshape(v.shape), -1, axis)


WIDE = False


def mx_kscale(k):
    if not WIDE:
        return np.ones(k)
    levels = np.array([10, -10, 5, -5, 0])
    if k % 512:
        return np.exp2(np.random.permutation(np.resize(levels, k // 32))).repeat(32)
    a = np.empty((k // 512, 16))
    for p in range(k // 512):
        a[p, :8] = np.random.permutation(np.resize(levels, 8))
        for g in range(8):
            far = levels[np.abs(levels - a[p, g]) >= 10]
            a[p, g + 8] = far[np.random.randint(len(far))]
    return np.exp2(a.ravel()).repeat(32)


def f64(x):
    return np.asarray(x).astype(np.float64)


def striped(idx):
    return np.tile(idx.reshape(-1, 16).T, (8, 1)).astype(np.uint16)


def unstriped(offs):
    return offs[:16].T.reshape(-1).astype(np.int64)


def pack_weight(w):
    k, n = w.shape
    w = f64(np.asarray(w, np.float32).astype(ml_dtypes.bfloat16)).reshape(k // 32, 32, n)
    amax = np.abs(w).max(1)
    byte = np.clip(np.where(amax > 0, np.frexp(amax)[1] - 1 + 127 - 7, 1), 1, 254)
    scaled = (w * np.exp2(127.0 - byte)[:, None, :]).reshape(k, n).astype(np.float32)
    words = np.ascontiguousarray(scaled.reshape(k // 512, 128, 4, n).transpose(0, 1, 3, 2)).astype(ml_dtypes.float8_e4m3fn).view(np.uint8)
    return words, np.ascontiguousarray(byte.astype(np.uint8).reshape(k // 512, 16, n))


def unpack_weight(words, scales):
    g, p, n, _ = words.shape
    vals = np.ascontiguousarray(words).view(ml_dtypes.float8_e4m3fn).astype(np.float64) * np.repeat(np.exp2(scales.astype(np.float64) - 127.0), 8, axis=1)[..., None]
    return vals.transpose(0, 1, 3, 2).reshape(g * 512, n)


K, T, S, N, V = 1024, 1024, 512, 256, 256
P = 2 ** 7


def setup_inputs():
    n = np.random.standard_normal
    s = mx_kscale(K)[:, None]
    packed_xT = pack_weight(n((K, T)) * s)
    return {
        "x_words": packed_xT[0],
        "x_scales": packed_xT[1],
        "w1": (n((K, N)) / np.sqrt(K) / s).astype(np.float32),
        "inv": (np.tile(np.random.uniform(0.3, 1.5, S), (P, 1))).astype(np.float32),
        "cnt": (np.tile(np.floor(np.random.uniform(1.0, 9.0, S)), (P, 1))).astype(np.float32),
        "offs": striped(np.random.permutation(T)[:S]),
        "pos1": striped(np.random.permutation(S)[:V]),
        "pos2": striped(np.random.permutation(S)[:V]),
        "pos3": striped(np.random.permutation(S)[:V]),
    }


def reference(x_words, x_scales, w1, inv, cnt, offs, pos1, pos2, pos3):
    xq = unpack_weight(x_words, x_scales)[:, unstriped(offs)]
    y = mxq(f64(w1), 0, "e4m3").T @ xq
    tgt = np.log(np.exp(y) + 1.0)
    res = tgt * (f64(inv)[:1] * f64(cnt)[:1])
    g0 = res[:, unstriped(pos1)]
    g1 = res[:, unstriped(pos2)]
    g2 = res[:, unstriped(pos3)]
    tot = g0 + g1 + g2
    return (np.maximum(np.maximum(g0, g1), g2)) / tot

@@ -1,0 +1,256 @@
+import math
+from contextlib import ExitStack
+
+import concourse.mybir as mybir
+from concourse.masks import make_identity
+
+K, T, S, N, V = 1024, 1024, 512, 256, 256
+FLOPS = 2 * K * S * N
+
+F32 = mybir.dt.float32
+BF16 = mybir.dt.bfloat16
+I32 = mybir.dt.int32
+U32 = mybir.dt.uint32
+U16 = mybir.dt.uint16
+U8 = mybir.dt.uint8
+FP8X4 = mybir.dt.float8_e4m3fn_x4
+ALU = mybir.AluOpType
+ACT = mybir.ActivationFunctionType
+
+P = 128
+PACK = 4
+K_PASS = P * PACK
+PASSES = K // K_PASS
+J_BLOCKS = S // P
+M_TILES = N // P
+LIST_ROWS = 16
+EXP_CAP = 2.0 ** 60
+Y_CAP = 60 * math.log(2.0)
+VECTOR_COLS = 160
+
+
+def interleave(copy, grouped, raw, cols):
+    copy(
+        out=grouped[:, cols, :].rearrange("p (c i) t -> p c t i", i=4),
+        in_=raw[:, :, cols].rearrange("p t (c i) -> p c t i", i=4),
+    )
+
+
+def tile_picked_yrestir_prob_p_kernel(
+    tc, x_words, x_scales, w1, inv, cnt, offs, pos1, pos2, pos3, out
+):
+    nc = tc.nc
+    with ExitStack() as ctx:
+        keep = ctx.enter_context(tc.tile_pool(name="keep", bufs=1))
+        psum = ctx.enter_context(tc.psum_pool(name="psum", bufs=1))
+
+        def bank(tag, shape, name):
+            return psum.tile(shape, F32, tag=tag, name=name)
+
+        picked = keep.tile([P, S // LIST_ROWS], U16)
+        nc.sync.dma_start(picked[:], offs)
+
+        scale_rows = keep.tile([P, T // 4], I32)
+        scale_table = keep.tile([P, T], U8, tag="codes0", align_bytes=64)
+        nc.vector.memset(scale_table[:].bitcast(I32), 0)
+
+        def load_scales(q):
+            live = slice(32 * q, 32 * q + 4 * PASSES)
+            nc.sync.dma_start(scale_rows[live, :], x_scales[:, 4 * q : 4 * q + 4, :].bitcast(I32))
+            nc.vector.tensor_copy(scale_table[live, :].bitcast(I32), scale_rows[live, :])
+
+        word_tables = [keep.tile([P, T], I32, name="word_table%d" % o, tag="table%d" % o, align_bytes=64) for o in range(PASSES)]
+        w_raw = [keep.tile([P, PACK, N], F32, name="w_raw%d" % o) for o in range(PASSES)]
+
+        def load_words(o):
+            nc.sync.dma_start(word_tables[o][:], x_words[o].rearrange("p n t -> p (n t)").bitcast(I32))
+
+        def load_w(o):
+            rows = w1[o * K_PASS : (o + 1) * K_PASS, :]
+            nc.sync.dma_start(w_raw[o][:], rows.rearrange("(p t) n -> p t n", t=PACK))
+
+        inv_rows = keep.tile([P, J_BLOCKS], F32)
+        cnt_rows = keep.tile([P, J_BLOCKS], F32)
+        for q in range(4):
+            load_scales(q)
+        load_words(0)
+        load_w(0)
+        load_w(1)
+        load_words(1)
+        with nc.allow_non_contiguous_dma(reason="one value a partition"):
+            nc.sync.dma_start(inv_rows[:], inv[0:1, :].rearrange("o (b p) -> p (o b)", p=P))
+            nc.sync.dma_start(cnt_rows[:], cnt[0:1, :].rearrange("o (b p) -> p (o b)", p=P))
+        places = []
+        for i, pos in enumerate((pos1, pos2, pos3)):
+            place = keep.tile([P, V // LIST_ROWS], U16, name="place%d" % i)
+            nc.sync.dma_start(place[:], pos)
+            places.append(place)
+
+        ident = keep.tile([P, P], F32)
+        make_identity(nc, ident[:])
+
+        x_scale = keep.tile([P, S], U8, align_bytes=64)
+        x_codes = []
+        w_grouped = []
+        w_codes = [keep.tile([P, N], U32, name="w_codes%d" % o, align_bytes=64) for o in range(PASSES)]
+        w_scale = [keep.tile([P, N], U8, name="w_scale%d" % o, align_bytes=64) for o in range(PASSES)]
+
+        def gather_words(o, first, last):
+            entries = picked[:, first // LIST_ROWS : last // LIST_ROWS]
+            nc.vector.tensor_copy(x_codes[o][:, first:last], word_tables[o][:].bitcast(U32).indirect(entries))
+
+        def quantize_w(o):
+            nc.vector.quantize_mx(
+                out=w_codes[o][:].bitcast(FP8X4),
+                scales=w_scale[o][:],
+                in_=w_grouped[o][:].rearrange("p n t -> p (n t)"),
+            )
+
+        y = [bank("y%d" % b, [P, N], "y%d" % b) for b in range(J_BLOCKS)]
+
+        def multiply(o, b):
+            cols = slice(b * P, (b + 1) * P)
+            nc.tensor.matmul_mx(
+                out=y[b][:],
+                lhsT=x_codes[o][:, cols].bitcast(FP8X4),
+                lhsT_scale=x_scale[4 * o : P, cols],
+                rhs=w_codes[o][:].bitcast(FP8X4),
+                rhs_scale=w_scale[o][:],
+                start=(o == 0),
+                stop=(o == PASSES - 1),
+            )
+
+        nc.vector.tensor_copy(x_scale[:], scale_table[:].indirect(picked[:]))
+        x_codes.append(keep.tile([P, S], U32, name="x_codes0", tag="codes0", align_bytes=64))
+        gather_words(0, 0, S)
+        w_grouped.append(keep.tile([P, N, PACK], BF16, name="w_grouped0", align_bytes=64))
+        w_grouped.append(keep.tile([P, N, PACK], BF16, name="w_grouped1", tag="table0", align_bytes=64))
+        interleave(nc.scalar.copy, w_grouped[0], w_raw[0], slice(0, N))
+        quantize_w(0)
+        for b in range(J_BLOCKS):
+            multiply(0, b)
+        interleave(nc.vector.tensor_copy, w_grouped[1], w_raw[1], slice(0, VECTOR_COLS))
+        interleave(nc.scalar.copy, w_grouped[1], w_raw[1], slice(VECTOR_COLS, N))
+        quantize_w(1)
+        x_codes.append(keep.tile([P, S], U32, name="x_codes1", tag="table0", align_bytes=64))
+
+        exp_y = keep.tile([P, J_BLOCKS, N], F32)
+        for b in range(J_BLOCKS):
+            gather_words(1, b * P, (b + 1) * P)
+            multiply(1, b)
+            nc.scalar.activation(exp_y[:, b, :], y[b][:], ACT.Exp)
+
+        ln_in = [keep.tile([P, J_BLOCKS, P], F32, name="ln_in%d" % mt, tag="ln_in%d" % mt) for mt in range(M_TILES)]
+        for h in range(2):
+            for mt in range(M_TILES):
+                nc.vector.tensor_scalar(
+                    ln_in[mt][:, 2 * h : 2 * h + 2, :],
+                    exp_y[:, 2 * h : 2 * h + 2, mt * P : (mt + 1) * P],
+                    EXP_CAP,
+                    1.0,
+                    ALU.min,
+                    ALU.add,
+                )
+
+        weight = keep.tile([P, J_BLOCKS], F32, tag="table1", align_bytes=64)
+        nc.vector.tensor_tensor(weight[:], inv_rows[:], cnt_rows[:], ALU.mult)
+
+        y_w = keep.tile([P, J_BLOCKS, P], F32)
+        for b in range(J_BLOCKS):
+            nc.vector.tensor_scalar(y_w[:, b, :], y[b][:, 0:P], weight[:, b : b + 1], None, ALU.mult)
+
+        excess = keep.tile([P, J_BLOCKS, P], F32)
+        excess_w = keep.tile([P, J_BLOCKS, P], F32)
+        for b in range(J_BLOCKS):
+            nc.vector.tensor_scalar(excess[:, b, :], y[b][:, P:N], -Y_CAP, 0.0, ALU.add, ALU.max)
+        for b in range(J_BLOCKS):
+            nc.vector.tensor_scalar(excess_w[:, b, :], excess[:, b, :], weight[:, b : b + 1], None, ALU.mult)
+
+        res_turned = [bank("res%d" % mt, [P, S], "res_turned%d" % mt) for mt in range(M_TILES)]
+        target = [
+            keep.tile([P, J_BLOCKS, P], F32, name="target0", tag="table0", align_bytes=64),
+            keep.tile([P, J_BLOCKS, P], F32, name="target1"),
+        ]
+        target_w = [keep.tile([P, J_BLOCKS, P], F32, name="target_w%d" % mt, tag="target_w%d" % mt) for mt in range(M_TILES)]
+        res = [keep.tile([P, S], F32, name="res_sb%d" % mt, tag="res_sb%d" % mt) for mt in range(M_TILES)]
+
+        for h in range(2):
+            nc.scalar.activation(target[0][:, 2 * h : 2 * h + 2, :], ln_in[0][:, 2 * h : 2 * h + 2, :], ACT.Ln)
+        for b in range(J_BLOCKS):
+            nc.vector.scalar_tensor_tensor(
+                target_w[0][:, b, :], target[0][:, b, :], weight[:, b : b + 1], y_w[:, b, :], ALU.mult, ALU.max
+            )
+            nc.tensor.transpose(res_turned[0][:, b * P : (b + 1) * P], target_w[0][:, b, :], ident[:])
+        nc.vector.tensor_copy(res[0][:], res_turned[0][:])
+
+        nc.scalar.activation(target[1][:], ln_in[1][:], ACT.Ln)
+        for b in range(J_BLOCKS):
+            nc.scalar.activation(target_w[1][:, b, :], target[1][:, b, :], ACT.Copy, scale=weight[:, b : b + 1])
+        for part, first in ((excess_w, True), (target_w[1], False)):
+            for b in range(J_BLOCKS):
+                nc.tensor.matmul(
+                    res_turned[1][:, b * P : (b + 1) * P],
+                    part[:, b, :],
+                    ident[:],
+                    start=(first and b == 0),
+                    stop=(not first and b == J_BLOCKS - 1),
+                    is_transpose=True,
+                )
+        nc.scalar.copy(res[1][:], res_turned[1][:])
+
+        g = [keep.tile([P, 3, V], F32, name="g%d" % mt) for mt in range(M_TILES)]
+
+        def fetch(mt, i, cols):
+            entries = places[i][:, cols.start // LIST_ROWS : cols.stop // LIST_ROWS]
+            nc.vector.tensor_copy(g[mt][:, i, cols], res[mt][:].indirect(entries))
+
+        def inverse_of(total, width, name):
+            root = keep.tile([P, width], F32, name="root" + name, tag="root")
+            inverse = keep.tile([P, width], F32, name="inverse" + name)
+            nc.scalar.activation(root[:], total, ACT.Abs_reciprocal_sqrt)
+            nc.scalar.activation(inverse[:], root[:], ACT.Square)
+            return inverse
+
+        def sum_on_tensor(mt, cols, sum_tag, back_tag):
+            width = cols.stop - cols.start
+            blocks = width // P
+            total = bank(sum_tag, [P, width], "total%d" % mt)
+            for i in range(3):
+                fetch(mt, i, cols)
+                for c in range(blocks):
+                    nc.tensor.matmul(
+                        total[:, c * P : (c + 1) * P],
+                        g[mt][:, i, cols.start + c * P : cols.start + (c + 1) * P],
+                        ident[:],
+                        start=(i == 0 and c == 0),
+                        stop=(i == 2 and c == blocks - 1),
+                        is_transpose=True,
+                    )
+            inverse = inverse_of(total[:], width, "%d" % mt)
+            back = bank(back_tag, [P, width], "back%d" % mt)
+            for c in range(blocks):
+                nc.tensor.transpose(back[:, c * P : (c + 1) * P], inverse[:, c * P : (c + 1) * P], ident[:])
+            return back
+
+        whole, early, late = slice(0, V), slice(0, P), slice(P, V)
+        inverse0 = sum_on_tensor(0, whole, "res1", "y1")
+        inverse1 = sum_on_tensor(1, early, "y2", "y3")
+        pair_sum = keep.tile([P, P], F32, tag="pair")
+        total = keep.tile([P, P], F32)
+        fetch(1, 0, late)
+        fetch(1, 1, late)
+        fetch(1, 2, late)
+        nc.vector.tensor_tensor(pair_sum[:], g[1][:, 0, late], g[1][:, 1, late], ALU.add)
+        nc.vector.tensor_tensor(total[:], pair_sum[:], g[1][:, 2, late], ALU.add)
+        inverse2 = inverse_of(total[:], P, "2")
+
+        pair_max = keep.tile([P, M_TILES, V], F32, tag="pair")
+        largest = keep.tile([P, M_TILES, V], F32)
+        for mt in range(M_TILES):
+            nc.vector.tensor_tensor(pair_max[:, mt, :], g[mt][:, 0, :], g[mt][:, 1, :], ALU.max)
+        for mt in range(M_TILES):
+            nc.vector.tensor_tensor(largest[:, mt, :], pair_max[:, mt, :], g[mt][:, 2, :], ALU.max)
+        for n, (mt, cols, inverse) in enumerate(((0, whole, inverse0), (1, early, inverse1), (1, late, inverse2))):
+            result = keep.tile([P, cols.stop - cols.start], F32, name="result%d" % n)
+            nc.vector.tensor_tensor(result[:], largest[:, mt, cols], inverse[:], ALU.mult)
+            nc.sync.dma_start(out[mt * P : (mt + 1) * P, cols], result[:])

@@ -69,17 +69,16 @@ def tile_picked_yrestir_prob_p_kernel(
             rows = w1[o * K_PASS : (o + 1) * K_PASS, :]
             nc.sync.dma_start(w_raw[o][:], rows.rearrange("(p t) n -> p t n", t=PACK))
 
-        inv_rows = keep.tile([P, J_BLOCKS], F32)
-        cnt_rows = keep.tile([P, J_BLOCKS], F32)
+        inv_rows = keep.tile([J_BLOCKS, P], F32)
+        cnt_rows = keep.tile([J_BLOCKS, P], F32)
         for q in range(4):
             load_scales(q)
         load_words(0)
         load_w(0)
         load_w(1)
         load_words(1)
-        with nc.allow_non_contiguous_dma(reason="one value a partition"):
-            nc.sync.dma_start(inv_rows[:], inv[0:1, :].rearrange("o (b p) -> p (o b)", p=P))
-            nc.sync.dma_start(cnt_rows[:], cnt[0:1, :].rearrange("o (b p) -> p (o b)", p=P))
+        nc.sync.dma_start(inv_rows[:], inv[0:1, :].rearrange("o (b p) -> (o b) p", p=P))
+        nc.sync.dma_start(cnt_rows[:], cnt[0:1, :].rearrange("o (b p) -> (o b) p", p=P))
         places = []
         for i, pos in enumerate((pos1, pos2, pos3)):
             place = keep.tile([P, V // LIST_ROWS], U16, name="place%d" % i)
@@ -110,15 +109,20 @@ def tile_picked_yrestir_prob_p_kernel(
 
         def multiply(o, b):
             cols = slice(b * P, (b + 1) * P)
-            nc.tensor.matmul_mx(
-                out=y[b][:],
-                lhsT=x_codes[o][:, cols].bitcast(FP8X4),
-                lhsT_scale=x_scale[4 * o : P, cols],
-                rhs=w_codes[o][:].bitcast(FP8X4),
-                rhs_scale=w_scale[o][:],
-                start=(o == 0),
-                stop=(o == PASSES - 1),
-            )
+            x_side = (x_codes[o][:, cols].bitcast(FP8X4), x_scale[4 * o : P, cols])
+            for mt in range(M_TILES):
+                rows = slice(mt * P, (mt + 1) * P)
+                w_side = (w_codes[o][:, rows].bitcast(FP8X4), w_scale[o][:, rows])
+                still, moving = (w_side, x_side) if mt == 0 else (x_side, w_side)
+                nc.tensor.matmul_mx(
+                    out=y[b][:, rows],
+                    lhsT=still[0],
+                    lhsT_scale=still[1],
+                    rhs=moving[0],
+                    rhs_scale=moving[1],
+                    start=(o == 0 and mt == 0),
+                    stop=(o == PASSES - 1 and mt == M_TILES - 1),
+                )
 
         nc.vector.tensor_copy(x_scale[:], scale_table[:].indirect(picked[:]))
         x_codes.append(keep.tile([P, S], U32, name="x_codes0", tag="codes0", align_bytes=64))
@@ -140,63 +144,60 @@ def tile_picked_yrestir_prob_p_kernel(
             multiply(1, b)
             nc.scalar.activation(exp_y[:, b, :], y[b][:], ACT.Exp)
 
-        ln_in = [keep.tile([P, J_BLOCKS, P], F32, name="ln_in%d" % mt, tag="ln_in%d" % mt) for mt in range(M_TILES)]
+        ln_in = keep.tile([P, J_BLOCKS, N], F32)
         for h in range(2):
-            for mt in range(M_TILES):
-                nc.vector.tensor_scalar(
-                    ln_in[mt][:, 2 * h : 2 * h + 2, :],
-                    exp_y[:, 2 * h : 2 * h + 2, mt * P : (mt + 1) * P],
-                    EXP_CAP,
-                    1.0,
-                    ALU.min,
-                    ALU.add,
-                )
+            pair = slice(2 * h, 2 * h + 2)
+            nc.vector.tensor_scalar(ln_in[:, pair, :], exp_y[:, pair, :], EXP_CAP, 1.0, ALU.min, ALU.add)
 
-        weight = keep.tile([P, J_BLOCKS], F32, tag="table1", align_bytes=64)
-        nc.vector.tensor_tensor(weight[:], inv_rows[:], cnt_rows[:], ALU.mult)
-
-        y_w = keep.tile([P, J_BLOCKS, P], F32)
+        weight_rows = keep.tile([P, P], F32, tag="table1", align_bytes=64)
+        nc.vector.memset(weight_rows[:], 0.0)
+        nc.vector.tensor_tensor(weight_rows[0:J_BLOCKS, :], inv_rows[:], cnt_rows[:], ALU.mult)
+        weight_turned = bank("spare0", [P, P], "weight_turned")
+        nc.tensor.transpose(weight_turned[:], weight_rows[:], ident[:])
+        weight = keep.tile([P, J_BLOCKS], F32)
+        nc.vector.tensor_copy(weight[:], weight_turned[:, 0:J_BLOCKS])
+        weight_wide = bank("spare1", [P, S], "weight_wide")
         for b in range(J_BLOCKS):
-            nc.vector.tensor_scalar(y_w[:, b, :], y[b][:, 0:P], weight[:, b : b + 1], None, ALU.mult)
+            nc.tensor.transpose(
+                weight_wide[:, b * P : (b + 1) * P], weight[:, b : b + 1].to_broadcast([P, P]), ident[:]
+            )
 
-        excess = keep.tile([P, J_BLOCKS, P], F32)
+        excess = keep.tile([P, J_BLOCKS, P], F32, tag="target0")
         excess_w = keep.tile([P, J_BLOCKS, P], F32)
         for b in range(J_BLOCKS):
             nc.vector.tensor_scalar(excess[:, b, :], y[b][:, P:N], -Y_CAP, 0.0, ALU.add, ALU.max)
         for b in range(J_BLOCKS):
             nc.vector.tensor_scalar(excess_w[:, b, :], excess[:, b, :], weight[:, b : b + 1], None, ALU.mult)
 
-        res_turned = [bank("res%d" % mt, [P, S], "res_turned%d" % mt) for mt in range(M_TILES)]
-        target = [
-            keep.tile([P, J_BLOCKS, P], F32, name="target0", tag="table0", align_bytes=64),
-            keep.tile([P, J_BLOCKS, P], F32, name="target1"),
-        ]
-        target_w = [keep.tile([P, J_BLOCKS, P], F32, name="target_w%d" % mt, tag="target_w%d" % mt) for mt in range(M_TILES)]
-        res = [keep.tile([P, S], F32, name="res_sb%d" % mt, tag="res_sb%d" % mt) for mt in range(M_TILES)]
-
+        res = [keep.tile([P, S], F32, name="res%d" % mt, tag="res%d" % mt) for mt in range(M_TILES)]
+        capped0 = keep.tile([P, J_BLOCKS, P], F32, tag="table0", align_bytes=64)
+        target0 = keep.tile([P, S], F32, tag="target0")
+        halves = (slice(0, S // 2), slice(S // 2, S))
         for h in range(2):
-            nc.scalar.activation(target[0][:, 2 * h : 2 * h + 2, :], ln_in[0][:, 2 * h : 2 * h + 2, :], ACT.Ln)
+            pair = slice(2 * h, 2 * h + 2)
+            nc.scalar.activation(capped0[:, pair, :], ln_in[:, pair, 0:P], ACT.Ln)
         for b in range(J_BLOCKS):
-            nc.vector.scalar_tensor_tensor(
-                target_w[0][:, b, :], target[0][:, b, :], weight[:, b : b + 1], y_w[:, b, :], ALU.mult, ALU.max
-            )
-            nc.tensor.transpose(res_turned[0][:, b * P : (b + 1) * P], target_w[0][:, b, :], ident[:])
-        nc.vector.tensor_copy(res[0][:], res_turned[0][:])
+            nc.vector.tensor_tensor(target0[:, b * P : (b + 1) * P], y[b][:, 0:P], capped0[:, b, :], ALU.max)
+        for half in halves:
+            nc.vector.tensor_tensor(res[0][:, half], target0[:, half], weight_wide[:, half], ALU.mult)
 
-        nc.scalar.activation(target[1][:], ln_in[1][:], ACT.Ln)
+        capped1 = keep.tile([P, J_BLOCKS, P], F32)
+        capped1_w = keep.tile([P, J_BLOCKS, P], F32)
+        res1_turned = bank("res1", [P, S], "res1_turned")
+        nc.scalar.activation(capped1[:], ln_in[:, :, P:N], ACT.Ln)
         for b in range(J_BLOCKS):
-            nc.scalar.activation(target_w[1][:, b, :], target[1][:, b, :], ACT.Copy, scale=weight[:, b : b + 1])
-        for part, first in ((excess_w, True), (target_w[1], False)):
+            nc.scalar.activation(capped1_w[:, b, :], capped1[:, b, :], ACT.Copy, scale=weight[:, b : b + 1])
+        for part, first in ((excess_w, True), (capped1_w, False)):
             for b in range(J_BLOCKS):
                 nc.tensor.matmul(
-                    res_turned[1][:, b * P : (b + 1) * P],
+                    res1_turned[:, b * P : (b + 1) * P],
                     part[:, b, :],
                     ident[:],
                     start=(first and b == 0),
                     stop=(not first and b == J_BLOCKS - 1),
                     is_transpose=True,
                 )
-        nc.scalar.copy(res[1][:], res_turned[1][:])
+        nc.scalar.copy(res[1][:], res1_turned[:])
 
         g = [keep.tile([P, 3, V], F32, name="g%d" % mt) for mt in range(M_TILES)]
 
@@ -204,47 +205,48 @@ def tile_picked_yrestir_prob_p_kernel(
             entries = places[i][:, cols.start // LIST_ROWS : cols.stop // LIST_ROWS]
             nc.vector.tensor_copy(g[mt][:, i, cols], res[mt][:].indirect(entries))
 
-        def inverse_of(total, width, name):
-            root = keep.tile([P, width], F32, name="root" + name, tag="root")
-            inverse = keep.tile([P, width], F32, name="inverse" + name)
-            nc.scalar.activation(root[:], total, ACT.Abs_reciprocal_sqrt)
-            nc.scalar.activation(inverse[:], root[:], ACT.Square)
+        def add_turned(total, mt, i, cols, start, stop):
+            for c in range(cols.start // P, cols.stop // P):
+                nc.tensor.matmul(
+                    total[:, c * P - cols.start : (c + 1) * P - cols.start],
+                    g[mt][:, i, c * P : (c + 1) * P],
+                    ident[:],
+                    start=(start and c == cols.start // P),
+                    stop=(stop and c == cols.stop // P - 1),
+                    is_transpose=True,
+                )
+
+        def inverse_of(total, tag, name):
+            width = total.shape[1]
+            root = keep.tile([P, width], F32, name="root" + name)
+            square = keep.tile([P, width], F32, name="square" + name)
+            nc.scalar.activation(root[:], total[:], ACT.Abs_reciprocal_sqrt)
+            nc.scalar.activation(square[:], root[:], ACT.Square)
+            inverse = bank(tag, [P, width], "inverse" + name)
+            for c in range(width // P):
+                nc.tensor.transpose(inverse[:, c * P : (c + 1) * P], square[:, c * P : (c + 1) * P], ident[:])
             return inverse
 
-        def sum_on_tensor(mt, cols, sum_tag, back_tag):
-            width = cols.stop - cols.start
-            blocks = width // P
-            total = bank(sum_tag, [P, width], "total%d" % mt)
-            for i in range(3):
-                fetch(mt, i, cols)
-                for c in range(blocks):
-                    nc.tensor.matmul(
-                        total[:, c * P : (c + 1) * P],
-                        g[mt][:, i, cols.start + c * P : cols.start + (c + 1) * P],
-                        ident[:],
-                        start=(i == 0 and c == 0),
-                        stop=(i == 2 and c == blocks - 1),
-                        is_transpose=True,
-                    )
-            inverse = inverse_of(total[:], width, "%d" % mt)
-            back = bank(back_tag, [P, width], "back%d" % mt)
-            for c in range(blocks):
-                nc.tensor.transpose(back[:, c * P : (c + 1) * P], inverse[:, c * P : (c + 1) * P], ident[:])
-            return back
-
         whole, early, late = slice(0, V), slice(0, P), slice(P, V)
-        inverse0 = sum_on_tensor(0, whole, "res1", "y1")
-        inverse1 = sum_on_tensor(1, early, "y2", "y3")
-        pair_sum = keep.tile([P, P], F32, tag="pair")
-        total = keep.tile([P, P], F32)
-        fetch(1, 0, late)
-        fetch(1, 1, late)
+        total0 = bank("res1", [P, V], "total0")
+        for i in range(3):
+            fetch(0, i, whole)
+            add_turned(total0, 0, i, whole, i == 0, i == 2)
+        inverse0 = inverse_of(total0, "y1", "0")
+        total1 = bank("y2", [P, P], "total1")
+        total2 = bank("y0", [P, P], "total2")
+        for i in range(2):
+            fetch(1, i, whole)
+            add_turned(total1, 1, i, early, i == 0, False)
+            add_turned(total2, 1, i, late, i == 0, False)
+        fetch(1, 2, early)
+        add_turned(total1, 1, 2, early, False, True)
         fetch(1, 2, late)
-        nc.vector.tensor_tensor(pair_sum[:], g[1][:, 0, late], g[1][:, 1, late], ALU.add)
-        nc.vector.tensor_tensor(total[:], pair_sum[:], g[1][:, 2, late], ALU.add)
-        inverse2 = inverse_of(total[:], P, "2")
+        add_turned(total2, 1, 2, late, False, True)
+        inverse1 = inverse_of(total1, "y3", "1")
+        inverse2 = inverse_of(total2, "spare0", "2")
 
-        pair_max = keep.tile([P, M_TILES, V], F32, tag="pair")
+        pair_max = keep.tile([P, M_TILES, V], F32, tag="res1")
         largest = keep.tile([P, M_TILES, V], F32)
         for mt in range(M_TILES):
             nc.vector.tensor_tensor(pair_max[:, mt, :], g[mt][:, 0, :], g[mt][:, 1, :], ALU.max)

@@ -173,9 +173,8 @@ def tile_picked_yrestir_prob_p_kernel(
         capped0 = keep.tile([P, J_BLOCKS, P], F32, tag="table0", align_bytes=64)
         target0 = keep.tile([P, S], F32, tag="target0")
         halves = (slice(0, S // 2), slice(S // 2, S))
-        for h in range(2):
-            pair = slice(2 * h, 2 * h + 2)
-            nc.scalar.activation(capped0[:, pair, :], ln_in[:, pair, 0:P], ACT.Ln)
+        for b in range(J_BLOCKS):
+            nc.scalar.activation(capped0[:, b, :], ln_in[:, b, 0:P], ACT.Ln)
         for b in range(J_BLOCKS):
             nc.vector.tensor_tensor(target0[:, b * P : (b + 1) * P], y[b][:, 0:P], capped0[:, b, :], ALU.max)
         for half in halves:
@@ -199,29 +198,33 @@ def tile_picked_yrestir_prob_p_kernel(
                 )
         nc.scalar.copy(res[1][:], res1_turned[:])
 
-        g = [keep.tile([P, 3, V], F32, name="g%d" % mt) for mt in range(M_TILES)]
+        g = keep.tile([P, M_TILES, 3, V], F32)
 
         def fetch(mt, i, cols):
             entries = places[i][:, cols.start // LIST_ROWS : cols.stop // LIST_ROWS]
-            nc.vector.tensor_copy(g[mt][:, i, cols], res[mt][:].indirect(entries))
+            nc.vector.tensor_copy(g[:, mt, i, cols], res[mt][:].indirect(entries))
 
         def add_turned(total, mt, i, cols, start, stop):
             for c in range(cols.start // P, cols.stop // P):
                 nc.tensor.matmul(
                     total[:, c * P - cols.start : (c + 1) * P - cols.start],
-                    g[mt][:, i, c * P : (c + 1) * P],
+                    g[:, mt, i, c * P : (c + 1) * P],
                     ident[:],
                     start=(start and c == cols.start // P),
                     stop=(stop and c == cols.stop // P - 1),
                     is_transpose=True,
                 )
 
-        def inverse_of(total, tag, name):
+        def inverse_of(total, name):
             width = total.shape[1]
-            root = keep.tile([P, width], F32, name="root" + name)
+            root = keep.tile([P, width], F32, name="root" + name, tag="root1" if name == "1" else "root")
             square = keep.tile([P, width], F32, name="square" + name)
             nc.scalar.activation(root[:], total[:], ACT.Abs_reciprocal_sqrt)
             nc.scalar.activation(square[:], root[:], ACT.Square)
+            return square
+
+        def turned_back(square, tag, name):
+            width = square.shape[1]
             inverse = bank(tag, [P, width], "inverse" + name)
             for c in range(width // P):
                 nc.tensor.transpose(inverse[:, c * P : (c + 1) * P], square[:, c * P : (c + 1) * P], ident[:])
@@ -232,26 +235,27 @@ def tile_picked_yrestir_prob_p_kernel(
         for i in range(3):
             fetch(0, i, whole)
             add_turned(total0, 0, i, whole, i == 0, i == 2)
-        inverse0 = inverse_of(total0, "y1", "0")
+        square0 = inverse_of(total0, "0")
         total1 = bank("y2", [P, P], "total1")
-        total2 = bank("y0", [P, P], "total2")
+        pair_sum = keep.tile([P, P], F32)
+        total2 = keep.tile([P, P], F32)
         for i in range(2):
             fetch(1, i, whole)
             add_turned(total1, 1, i, early, i == 0, False)
-            add_turned(total2, 1, i, late, i == 0, False)
+        nc.vector.tensor_tensor(pair_sum[:], g[:, 1, 0, late], g[:, 1, 1, late], ALU.add)
         fetch(1, 2, early)
         add_turned(total1, 1, 2, early, False, True)
         fetch(1, 2, late)
-        add_turned(total2, 1, 2, late, False, True)
-        inverse1 = inverse_of(total1, "y3", "1")
-        inverse2 = inverse_of(total2, "spare0", "2")
+        nc.vector.tensor_tensor(total2[:], pair_sum[:], g[:, 1, 2, late], ALU.add)
+        inverse0 = turned_back(square0, "y1", "0")
+        inverse1 = turned_back(inverse_of(total1, "1"), "y3", "1")
+        inverse2 = inverse_of(total2, "2")
 
         pair_max = keep.tile([P, M_TILES, V], F32, tag="res1")
         largest = keep.tile([P, M_TILES, V], F32)
+        nc.vector.tensor_tensor(pair_max[:], g[:, :, 0, :], g[:, :, 1, :], ALU.max)
         for mt in range(M_TILES):
-            nc.vector.tensor_tensor(pair_max[:, mt, :], g[mt][:, 0, :], g[mt][:, 1, :], ALU.max)
-        for mt in range(M_TILES):
-            nc.vector.tensor_tensor(largest[:, mt, :], pair_max[:, mt, :], g[mt][:, 2, :], ALU.max)
+            nc.vector.tensor_tensor(largest[:, mt, :], pair_max[:, mt, :], g[:, mt, 2, :], ALU.max)
         for n, (mt, cols, inverse) in enumerate(((0, whole, inverse0), (1, early, inverse1), (1, late, inverse2))):
             result = keep.tile([P, cols.stop - cols.start], F32, name="result%d" % n)
             nc.vector.tensor_tensor(result[:], largest[:, mt, cols], inverse[:], ALU.mult)

@@ -26,7 +26,7 @@ M_TILES = N // P
 LIST_ROWS = 16
 EXP_CAP = 2.0 ** 60
 Y_CAP = 60 * math.log(2.0)
-VECTOR_COLS = 160
+VECTOR_COLS = 192
 
 
 def interleave(copy, grouped, raw, cols):
@@ -48,7 +48,6 @@ def tile_picked_yrestir_prob_p_kernel(
             return psum.tile(shape, F32, tag=tag, name=name)
 
         picked = keep.tile([P, S // LIST_ROWS], U16)
-        nc.sync.dma_start(picked[:], offs)
 
         scale_rows = keep.tile([P, T // 4], I32)
         scale_table = keep.tile([P, T], U8, tag="codes0", align_bytes=64)
@@ -73,6 +72,7 @@ def tile_picked_yrestir_prob_p_kernel(
         cnt_rows = keep.tile([J_BLOCKS, P], F32)
         for q in range(4):
             load_scales(q)
+        nc.sync.dma_start(picked[:], offs)
         load_words(0)
         load_w(0)
         load_w(1)
@@ -215,27 +215,26 @@ def tile_picked_yrestir_prob_p_kernel(
                     is_transpose=True,
                 )
 
-        def inverse_of(total, name):
-            width = total.shape[1]
-            root = keep.tile([P, width], F32, name="root" + name, tag="root1" if name == "1" else "root")
-            square = keep.tile([P, width], F32, name="square" + name)
-            nc.scalar.activation(root[:], total[:], ACT.Abs_reciprocal_sqrt)
-            nc.scalar.activation(square[:], root[:], ACT.Square)
-            return square
+        inverse = keep.tile([P, M_TILES, V], F32)
 
-        def turned_back(square, tag, name):
-            width = square.shape[1]
-            inverse = bank(tag, [P, width], "inverse" + name)
+        def root_of(total, tag, name):
+            root = keep.tile([P, total.shape[1]], F32, name="root" + name, tag=tag)
+            nc.scalar.activation(root[:], total[:], ACT.Abs_reciprocal_sqrt)
+            return root
+
+        def turned_back(root, tag, name):
+            width = root.shape[1]
+            back = bank(tag, [P, width], "back" + name)
             for c in range(width // P):
-                nc.tensor.transpose(inverse[:, c * P : (c + 1) * P], square[:, c * P : (c + 1) * P], ident[:])
-            return inverse
+                nc.tensor.transpose(back[:, c * P : (c + 1) * P], root[:, c * P : (c + 1) * P], ident[:])
+            return back
 
         whole, early, late = slice(0, V), slice(0, P), slice(P, V)
         total0 = bank("res1", [P, V], "total0")
         for i in range(3):
             fetch(0, i, whole)
             add_turned(total0, 0, i, whole, i == 0, i == 2)
-        square0 = inverse_of(total0, "0")
+        root0 = root_of(total0, "root0", "0")
         total1 = bank("y2", [P, P], "total1")
         pair_sum = keep.tile([P, P], F32)
         total2 = keep.tile([P, P], F32)
@@ -247,16 +246,19 @@ def tile_picked_yrestir_prob_p_kernel(
         add_turned(total1, 1, 2, early, False, True)
         fetch(1, 2, late)
         nc.vector.tensor_tensor(total2[:], pair_sum[:], g[:, 1, 2, late], ALU.add)
-        inverse0 = turned_back(square0, "y1", "0")
-        inverse1 = turned_back(inverse_of(total1, "1"), "y3", "1")
-        inverse2 = inverse_of(total2, "2")
+        root1 = root_of(total1, "root1", "1")
+        nc.scalar.activation(inverse[:, 0, :], turned_back(root0, "y1", "0")[:], ACT.Square)
+        root2 = root_of(total2, "root0", "2")
+        nc.scalar.activation(inverse[:, 1, early], turned_back(root1, "y3", "1")[:], ACT.Square)
+        nc.scalar.activation(inverse[:, 1, late], root2[:], ACT.Square)
 
         pair_max = keep.tile([P, M_TILES, V], F32, tag="res1")
         largest = keep.tile([P, M_TILES, V], F32)
-        nc.vector.tensor_tensor(pair_max[:], g[:, :, 0, :], g[:, :, 1, :], ALU.max)
+        result = keep.tile([P, M_TILES, V], F32)
+        for mt in range(M_TILES):
+            nc.vector.tensor_tensor(pair_max[:, mt, :], g[:, mt, 0, :], g[:, mt, 1, :], ALU.max)
         for mt in range(M_TILES):
             nc.vector.tensor_tensor(largest[:, mt, :], pair_max[:, mt, :], g[:, mt, 2, :], ALU.max)
-        for n, (mt, cols, inverse) in enumerate(((0, whole, inverse0), (1, early, inverse1), (1, late, inverse2))):
-            result = keep.tile([P, cols.stop - cols.start], F32, name="result%d" % n)
-            nc.vector.tensor_tensor(result[:], largest[:, mt, cols], inverse[:], ALU.mult)
-            nc.sync.dma_start(out[mt * P : (mt + 1) * P, cols], result[:])
+        for mt in range(M_TILES):
+            nc.vector.tensor_tensor(result[:, mt, :], largest[:, mt, :], inverse[:, mt, :], ALU.mult)
+            nc.sync.dma_start(out[mt * P : (mt + 1) * P, :], result[:, mt, :])

import math
from contextlib import ExitStack

import concourse.mybir as mybir
from concourse.masks import make_identity

K, T, S, N, V = 1024, 1024, 512, 256, 256
FLOPS = 2 * K * S * N

F32 = mybir.dt.float32
BF16 = mybir.dt.bfloat16
I32 = mybir.dt.int32
U32 = mybir.dt.uint32
U16 = mybir.dt.uint16
U8 = mybir.dt.uint8
FP8X4 = mybir.dt.float8_e4m3fn_x4
ALU = mybir.AluOpType
ACT = mybir.ActivationFunctionType

P = 128
PACK = 4
K_PASS = P * PACK
PASSES = K // K_PASS
J_BLOCKS = S // P
M_TILES = N // P
LIST_ROWS = 16
EXP_CAP = 2.0 ** 60
Y_CAP = 60 * math.log(2.0)
VECTOR_COLS = 192


def interleave(copy, grouped, raw, cols):
    copy(
        out=grouped[:, cols, :].rearrange("p (c i) t -> p c t i", i=4),
        in_=raw[:, :, cols].rearrange("p t (c i) -> p c t i", i=4),
    )


def tile_picked_yrestir_prob_p_kernel(
    tc, x_words, x_scales, w1, inv, cnt, offs, pos1, pos2, pos3, out
):
    nc = tc.nc
    with ExitStack() as ctx:
        keep = ctx.enter_context(tc.tile_pool(name="keep", bufs=1))
        psum = ctx.enter_context(tc.psum_pool(name="psum", bufs=1))

        def bank(tag, shape, name):
            return psum.tile(shape, F32, tag=tag, name=name)

        picked = keep.tile([P, S // LIST_ROWS], U16)

        scale_rows = keep.tile([P, T // 4], I32)
        scale_table = keep.tile([P, T], U8, tag="codes0", align_bytes=64)
        nc.vector.memset(scale_table[:].bitcast(I32), 0)

        def load_scales(q):
            live = slice(32 * q, 32 * q + 4 * PASSES)
            nc.sync.dma_start(scale_rows[live, :], x_scales[:, 4 * q : 4 * q + 4, :].bitcast(I32))
            nc.vector.tensor_copy(scale_table[live, :].bitcast(I32), scale_rows[live, :])

        word_tables = [keep.tile([P, T], I32, name="word_table%d" % o, tag="table%d" % o, align_bytes=64) for o in range(PASSES)]
        w_raw = [keep.tile([P, PACK, N], F32, name="w_raw%d" % o) for o in range(PASSES)]

        def load_words(o):
            nc.sync.dma_start(word_tables[o][:], x_words[o].rearrange("p n t -> p (n t)").bitcast(I32))

        def load_w(o):
            rows = w1[o * K_PASS : (o + 1) * K_PASS, :]
            nc.sync.dma_start(w_raw[o][:], rows.rearrange("(p t) n -> p t n", t=PACK))

        inv_rows = keep.tile([J_BLOCKS, P], F32)
        cnt_rows = keep.tile([J_BLOCKS, P], F32)
        for q in range(4):
            load_scales(q)
        nc.sync.dma_start(picked[:], offs)
        load_words(0)
        load_w(0)
        load_w(1)
        load_words(1)
        nc.sync.dma_start(inv_rows[:], inv[0:1, :].rearrange("o (b p) -> (o b) p", p=P))
        nc.sync.dma_start(cnt_rows[:], cnt[0:1, :].rearrange("o (b p) -> (o b) p", p=P))
        places = []
        for i, pos in enumerate((pos1, pos2, pos3)):
            place = keep.tile([P, V // LIST_ROWS], U16, name="place%d" % i)
            nc.sync.dma_start(place[:], pos)
            places.append(place)

        ident = keep.tile([P, P], F32)
        make_identity(nc, ident[:])

        x_scale = keep.tile([P, S], U8, align_bytes=64)
        x_codes = []
        w_grouped = []
        w_codes = [keep.tile([P, N], U32, name="w_codes%d" % o, align_bytes=64) for o in range(PASSES)]
        w_scale = [keep.tile([P, N], U8, name="w_scale%d" % o, align_bytes=64) for o in range(PASSES)]

        def gather_words(o, first, last):
            entries = picked[:, first // LIST_ROWS : last // LIST_ROWS]
            nc.vector.tensor_copy(x_codes[o][:, first:last], word_tables[o][:].bitcast(U32).indirect(entries))

        def quantize_w(o):
            nc.vector.quantize_mx(
                out=w_codes[o][:].bitcast(FP8X4),
                scales=w_scale[o][:],
                in_=w_grouped[o][:].rearrange("p n t -> p (n t)"),
            )

        y = [bank("y%d" % b, [P, N], "y%d" % b) for b in range(J_BLOCKS)]

        def multiply(o, b):
            cols = slice(b * P, (b + 1) * P)
            x_side = (x_codes[o][:, cols].bitcast(FP8X4), x_scale[4 * o : P, cols])
            for mt in range(M_TILES):
                rows = slice(mt * P, (mt + 1) * P)
                w_side = (w_codes[o][:, rows].bitcast(FP8X4), w_scale[o][:, rows])
                still, moving = (w_side, x_side) if mt == 0 else (x_side, w_side)
                nc.tensor.matmul_mx(
                    out=y[b][:, rows],
                    lhsT=still[0],
                    lhsT_scale=still[1],
                    rhs=moving[0],
                    rhs_scale=moving[1],
                    start=(o == 0 and mt == 0),
                    stop=(o == PASSES - 1 and mt == M_TILES - 1),
                )

        nc.vector.tensor_copy(x_scale[:], scale_table[:].indirect(picked[:]))
        x_codes.append(keep.tile([P, S], U32, name="x_codes0", tag="codes0", align_bytes=64))
        gather_words(0, 0, S)
        w_grouped.append(keep.tile([P, N, PACK], BF16, name="w_grouped0", align_bytes=64))
        w_grouped.append(keep.tile([P, N, PACK], BF16, name="w_grouped1", tag="table0", align_bytes=64))
        interleave(nc.scalar.copy, w_grouped[0], w_raw[0], slice(0, N))
        quantize_w(0)
        for b in range(J_BLOCKS):
            multiply(0, b)
        interleave(nc.vector.tensor_copy, w_grouped[1], w_raw[1], slice(0, VECTOR_COLS))
        interleave(nc.scalar.copy, w_grouped[1], w_raw[1], slice(VECTOR_COLS, N))
        quantize_w(1)
        x_codes.append(keep.tile([P, S], U32, name="x_codes1", tag="table0", align_bytes=64))

        exp_y = keep.tile([P, J_BLOCKS, N], F32)
        for b in range(J_BLOCKS):
            gather_words(1, b * P, (b + 1) * P)
            multiply(1, b)
            nc.scalar.activation(exp_y[:, b, :], y[b][:], ACT.Exp)

        ln_in = keep.tile([P, J_BLOCKS, N], F32)
        for h in range(2):
            pair = slice(2 * h, 2 * h + 2)
            nc.vector.tensor_scalar(ln_in[:, pair, :], exp_y[:, pair, :], EXP_CAP, 1.0, ALU.min, ALU.add)

        weight_rows = keep.tile([P, P], F32, tag="table1", align_bytes=64)
        nc.vector.memset(weight_rows[:], 0.0)
        nc.vector.tensor_tensor(weight_rows[0:J_BLOCKS, :], inv_rows[:], cnt_rows[:], ALU.mult)
        weight_turned = bank("spare0", [P, P], "weight_turned")
        nc.tensor.transpose(weight_turned[:], weight_rows[:], ident[:])
        weight = keep.tile([P, J_BLOCKS], F32)
        nc.vector.tensor_copy(weight[:], weight_turned[:, 0:J_BLOCKS])
        weight_wide = bank("spare1", [P, S], "weight_wide")
        for b in range(J_BLOCKS):
            nc.tensor.transpose(
                weight_wide[:, b * P : (b + 1) * P], weight[:, b : b + 1].to_broadcast([P, P]), ident[:]
            )

        excess = keep.tile([P, J_BLOCKS, P], F32, tag="target0")
        excess_w = keep.tile([P, J_BLOCKS, P], F32)
        for b in range(J_BLOCKS):
            nc.vector.tensor_scalar(excess[:, b, :], y[b][:, P:N], -Y_CAP, 0.0, ALU.add, ALU.max)
        for b in range(J_BLOCKS):
            nc.vector.tensor_scalar(excess_w[:, b, :], excess[:, b, :], weight[:, b : b + 1], None, ALU.mult)

        res = [keep.tile([P, S], F32, name="res%d" % mt, tag="res%d" % mt) for mt in range(M_TILES)]
        capped0 = keep.tile([P, J_BLOCKS, P], F32, tag="table0", align_bytes=64)
        target0 = keep.tile([P, S], F32, tag="target0")
        halves = (slice(0, S // 2), slice(S // 2, S))
        for b in range(J_BLOCKS):
            nc.scalar.activation(capped0[:, b, :], ln_in[:, b, 0:P], ACT.Ln)
        for b in range(J_BLOCKS):
            nc.vector.tensor_tensor(target0[:, b * P : (b + 1) * P], y[b][:, 0:P], capped0[:, b, :], ALU.max)
        for half in halves:
            nc.vector.tensor_tensor(res[0][:, half], target0[:, half], weight_wide[:, half], ALU.mult)

        capped1 = keep.tile([P, J_BLOCKS, P], F32)
        capped1_w = keep.tile([P, J_BLOCKS, P], F32)
        res1_turned = bank("res1", [P, S], "res1_turned")
        nc.scalar.activation(capped1[:], ln_in[:, :, P:N], ACT.Ln)
        for b in range(J_BLOCKS):
            nc.scalar.activation(capped1_w[:, b, :], capped1[:, b, :], ACT.Copy, scale=weight[:, b : b + 1])
        for part, first in ((excess_w, True), (capped1_w, False)):
            for b in range(J_BLOCKS):
                nc.tensor.matmul(
                    res1_turned[:, b * P : (b + 1) * P],
                    part[:, b, :],
                    ident[:],
                    start=(first and b == 0),
                    stop=(not first and b == J_BLOCKS - 1),
                    is_transpose=True,
                )
        nc.scalar.copy(res[1][:], res1_turned[:])

        g = keep.tile([P, M_TILES, 3, V], F32)

        def fetch(mt, i, cols):
            entries = places[i][:, cols.start // LIST_ROWS : cols.stop // LIST_ROWS]
            nc.vector.tensor_copy(g[:, mt, i, cols], res[mt][:].indirect(entries))

        def add_turned(total, mt, i, cols, start, stop):
            for c in range(cols.start // P, cols.stop // P):
                nc.tensor.matmul(
                    total[:, c * P - cols.start : (c + 1) * P - cols.start],
                    g[:, mt, i, c * P : (c + 1) * P],
                    ident[:],
                    start=(start and c == cols.start // P),
                    stop=(stop and c == cols.stop // P - 1),
                    is_transpose=True,
                )

        inverse = keep.tile([P, M_TILES, V], F32)

        def root_of(total, tag, name):
            root = keep.tile([P, total.shape[1]], F32, name="root" + name, tag=tag)
            nc.scalar.activation(root[:], total[:], ACT.Abs_reciprocal_sqrt)
            return root

        def turned_back(root, tag, name):
            width = root.shape[1]
            back = bank(tag, [P, width], "back" + name)
            for c in range(width // P):
                nc.tensor.transpose(back[:, c * P : (c + 1) * P], root[:, c * P : (c + 1) * P], ident[:])
            return back

        whole, early, late = slice(0, V), slice(0, P), slice(P, V)
        total0 = bank("res1", [P, V], "total0")
        for i in range(3):
            fetch(0, i, whole)
            add_turned(total0, 0, i, whole, i == 0, i == 2)
        root0 = root_of(total0, "root0", "0")
        total1 = bank("y2", [P, P], "total1")
        pair_sum = keep.tile([P, P], F32)
        total2 = keep.tile([P, P], F32)
        for i in range(2):
            fetch(1, i, whole)
            add_turned(total1, 1, i, early, i == 0, False)
        nc.vector.tensor_tensor(pair_sum[:], g[:, 1, 0, late], g[:, 1, 1, late], ALU.add)
        fetch(1, 2, early)
        add_turned(total1, 1, 2, early, False, True)
        fetch(1, 2, late)
        nc.vector.tensor_tensor(total2[:], pair_sum[:], g[:, 1, 2, late], ALU.add)
        root1 = root_of(total1, "root1", "1")
        nc.scalar.activation(inverse[:, 0, :], turned_back(root0, "y1", "0")[:], ACT.Square)
        root2 = root_of(total2, "root0", "2")
        nc.scalar.activation(inverse[:, 1, early], turned_back(root1, "y3", "1")[:], ACT.Square)
        nc.scalar.activation(inverse[:, 1, late], root2[:], ACT.Square)

        pair_max = keep.tile([P, M_TILES, V], F32, tag="res1")
        largest = keep.tile([P, M_TILES, V], F32)
        result = keep.tile([P, M_TILES, V], F32)
        for mt in range(M_TILES):
            nc.vector.tensor_tensor(pair_max[:, mt, :], g[:, mt, 0, :], g[:, mt, 1, :], ALU.max)
        for mt in range(M_TILES):
            nc.vector.tensor_tensor(largest[:, mt, :], pair_max[:, mt, :], g[:, mt, 2, :], ALU.max)
        for mt in range(M_TILES):
            nc.vector.tensor_tensor(result[:, mt, :], largest[:, mt, :], inverse[:, mt, :], ALU.mult)
            nc.sync.dma_start(out[mt * P : (mt + 1) * P, :], result[:, mt, :])
